import numpy as np
import ml_dtypes

BF16 = ml_dtypes.bfloat16


def bf(x):
    return np.asarray(x, np.float32).astype(BF16)


def f32(x):
    return np.asarray(x, np.float32)


def f64(x):
    return np.asarray(x).astype(np.float64)


def striped(idx):
    return np.concatenate([l.reshape(-1, 16).T for l in idx])


def rows(idx, k):
    return np.tile(np.repeat(idx, 16, axis=0), (k // (16 * 8), 1))


def look(tab, idx):
    return np.take_along_axis(f64(tab), rows(idx, len(tab)), axis=1)


K, S, V, N, M = 512, 2048, 2048, 2048, 512


def setup_inputs():
    return {"tab": f32(np.random.standard_normal((K, S))), "w": bf(np.random.standard_normal((K, M)) / np.sqrt(K)), "offs": striped(np.random.randint(0, S, (8, N)))}


def reference(tab, w, offs):
    idx = np.stack([g.T.reshape(-1) for g in np.split(offs, 8)])
    t = look(tab, idx)
    x = (t >= 0.25) * 0.5
    y = f64(w).T @ x
    return y

@@ -1,0 +1,53 @@
+import concourse.mybir as mybir
+
+F32, BF16, U16 = mybir.dt.float32, mybir.dt.bfloat16, mybir.dt.uint16
+ALU = mybir.AluOpType
+
+P = 128
+PIECE = 512
+GROUP = 16
+BANKS = 8
+THRESHOLD, LEVEL = 0.25, 0.5
+
+FLOPS = 2 * 512 * 512 * 2048
+
+
+def tile_lookup_deq_step_none_kernel(tc, tab, w, offs, out):
+    nc = tc.nc
+    (K, S), (M, N) = tab.shape, out.shape
+    blocks, pieces, strips = K // P, N // PIECE, M // P
+    columns = PIECE // GROUP
+    open_pieces = BANKS // strips
+
+    with (
+        tc.tile_pool(name="held", bufs=1) as held,
+        tc.tile_pool(name="staging", bufs=BANKS) as staging,
+        tc.psum_pool(name="psum", bufs=BANKS) as psum,
+    ):
+        offsets = held.tile([P, N // GROUP], U16, name="offsets")
+        nc.sync.dma_start(offsets[:], offs)
+        windows, weights = [], []
+        for r in range(blocks):
+            windows.append(held.tile([P, S], F32, name=f"window{r}"))
+            weights.append(held.tile([P, M], BF16, name=f"weights{r}"))
+            nc.sync.dma_start(windows[r][:], tab[r * P:(r + 1) * P, :])
+            nc.sync.dma_start(weights[r][:], w[r * P:(r + 1) * P, :])
+
+        order = [(r, j) for r in range(blocks) for j in range(open_pieces)]
+        order += [(r, j) for j in range(open_pieces, pieces) for r in range(blocks)]
+
+        sums = {}
+        for r, j in order:
+            x = held.tile([P, PIECE], F32, name=f"x{r}_{j}")
+            picked = windows[r][:].indirect(offsets[:, j * columns:(j + 1) * columns])
+            nc.vector.tensor_scalar(x[:], picked, THRESHOLD, LEVEL, ALU.is_ge, ALU.mult)
+            x_bf16 = x[:].bitcast(BF16)[:, 1::2]
+            for m in range(strips):
+                if r == 0:
+                    sums[j, m] = psum.tile([P, PIECE], F32, name="sums")
+                nc.tensor.matmul(sums[j, m][:], weights[r][:, m * P:(m + 1) * P], x_bf16,
+                                 start=(r == 0), stop=(r == blocks - 1))
+                if r == blocks - 1:
+                    staged = staging.tile([P, PIECE], F32, name="staged")
+                    nc.scalar.copy(staged[:], sums[j, m][:])
+                    nc.sync.dma_start(out[m * P:(m + 1) * P, j * PIECE:(j + 1) * PIECE], staged[:])

@@ -7,6 +7,7 @@ P = 128
 PIECE = 512
 GROUP = 16
 BANKS = 8
+RING = 3
 THRESHOLD, LEVEL = 0.25, 0.5
 
 FLOPS = 2 * 512 * 512 * 2048
@@ -22,7 +23,7 @@ def tile_lookup_deq_step_none_kernel(tc, tab, w, offs, out):
     with (
         tc.tile_pool(name="held", bufs=1) as held,
         tc.tile_pool(name="staging", bufs=BANKS) as staging,
-        tc.psum_pool(name="psum", bufs=BANKS) as psum,
+        tc.psum_pool(name="psum", bufs=1) as psum,
     ):
         offsets = held.tile([P, N // GROUP], U16, name="offsets")
         nc.sync.dma_start(offsets[:], offs)
@@ -34,20 +35,25 @@ def tile_lookup_deq_step_none_kernel(tc, tab, w, offs, out):
             nc.sync.dma_start(weights[r][:], w[r * P:(r + 1) * P, :])
 
         order = [(r, j) for r in range(blocks) for j in range(open_pieces)]
-        order += [(r, j) for j in range(open_pieces, pieces) for r in range(blocks)]
+        order += [(r, j) for j in range(open_pieces, pieces) for r in reversed(range(blocks))]
 
-        sums = {}
-        for r, j in order:
-            x = held.tile([P, PIECE], F32, name=f"x{r}_{j}")
+        ring = [held.tile([P, PIECE], F32, name=f"x{n}") for n in range(RING)]
+        banks = [psum.tile([P, PIECE], F32, name=f"bank{b}") for b in range(BANKS)]
+        done = [0] * pieces
+        for n, (r, j) in enumerate(order):
+            x = ring[n % RING]
+            done[j] += 1
             picked = windows[r][:].indirect(offsets[:, j * columns:(j + 1) * columns])
             nc.vector.tensor_scalar(x[:], picked, THRESHOLD, LEVEL, ALU.is_ge, ALU.mult)
             x_bf16 = x[:].bitcast(BF16)[:, 1::2]
             for m in range(strips):
-                if r == 0:
-                    sums[j, m] = psum.tile([P, PIECE], F32, name="sums")
-                nc.tensor.matmul(sums[j, m][:], weights[r][:, m * P:(m + 1) * P], x_bf16,
-                                 start=(r == 0), stop=(r == blocks - 1))
-                if r == blocks - 1:
+                sums = banks[(j % open_pieces) * strips + m]
+                nc.tensor.matmul(sums[:], weights[r][:, m * P:(m + 1) * P], x_bf16,
+                                 start=(done[j] == 1), stop=(done[j] == blocks))
+                if done[j] == blocks:
                     staged = staging.tile([P, PIECE], F32, name="staged")
-                    nc.scalar.copy(staged[:], sums[j, m][:])
+                    if j == pieces - 1 and m % 2 == 1:
+                        nc.vector.tensor_copy(staged[:], sums[:])
+                    else:
+                        nc.scalar.copy(staged[:], sums[:])
                     nc.sync.dma_start(out[m * P:(m + 1) * P, j * PIECE:(j + 1) * PIECE], staged[:])

@@ -8,6 +8,7 @@ PIECE = 512
 GROUP = 16
 BANKS = 8
 RING = 3
+WARM_UPS = 8
 THRESHOLD, LEVEL = 0.25, 0.5
 
 FLOPS = 2 * 512 * 512 * 2048
@@ -39,6 +40,14 @@ def tile_lookup_deq_step_none_kernel(tc, tab, w, offs, out):
 
         ring = [held.tile([P, PIECE], F32, name=f"x{n}") for n in range(RING)]
         banks = [psum.tile([P, PIECE], F32, name=f"bank{b}") for b in range(BANKS)]
+
+        zeros = held.tile([P, PIECE], BF16, name="zeros")
+        zero_weights = held.tile([P, P], BF16, name="zero_weights")
+        nc.vector.memset(zeros[:], 0.0)
+        nc.scalar.copy(zero_weights[:], zeros[:, :P])
+        for warm_up in range(WARM_UPS):
+            nc.tensor.matmul(banks[-1][:], zero_weights[:], zeros[:], start=True, stop=True)
+
         done = [0] * pieces
         for n, (r, j) in enumerate(order):
             x = ring[n % RING]

import concourse.mybir as mybir

F32, BF16, U16 = mybir.dt.float32, mybir.dt.bfloat16, mybir.dt.uint16
ALU = mybir.AluOpType

P = 128
PIECE = 512
GROUP = 16
BANKS = 8
RING = 3
WARM_UPS = 8
THRESHOLD, LEVEL = 0.25, 0.5

FLOPS = 2 * 512 * 512 * 2048


def tile_lookup_deq_step_none_kernel(tc, tab, w, offs, out):
    nc = tc.nc
    (K, S), (M, N) = tab.shape, out.shape
    blocks, pieces, strips = K // P, N // PIECE, M // P
    columns = PIECE // GROUP
    open_pieces = BANKS // strips

    with (
        tc.tile_pool(name="held", bufs=1) as held,
        tc.tile_pool(name="staging", bufs=BANKS) as staging,
        tc.psum_pool(name="psum", bufs=1) as psum,
    ):
        offsets = held.tile([P, N // GROUP], U16, name="offsets")
        nc.sync.dma_start(offsets[:], offs)
        windows, weights = [], []
        for r in range(blocks):
            windows.append(held.tile([P, S], F32, name=f"window{r}"))
            weights.append(held.tile([P, M], BF16, name=f"weights{r}"))
            nc.sync.dma_start(windows[r][:], tab[r * P:(r + 1) * P, :])
            nc.sync.dma_start(weights[r][:], w[r * P:(r + 1) * P, :])

        order = [(r, j) for r in range(blocks) for j in range(open_pieces)]
        order += [(r, j) for j in range(open_pieces, pieces) for r in reversed(range(blocks))]

        ring = [held.tile([P, PIECE], F32, name=f"x{n}") for n in range(RING)]
        banks = [psum.tile([P, PIECE], F32, name=f"bank{b}") for b in range(BANKS)]

        zeros = held.tile([P, PIECE], BF16, name="zeros")
        zero_weights = held.tile([P, P], BF16, name="zero_weights")
        nc.vector.memset(zeros[:], 0.0)
        nc.scalar.copy(zero_weights[:], zeros[:, :P])
        for warm_up in range(WARM_UPS):
            nc.tensor.matmul(banks[-1][:], zero_weights[:], zeros[:], start=True, stop=True)

        done = [0] * pieces
        for n, (r, j) in enumerate(order):
            x = ring[n % RING]
            done[j] += 1
            picked = windows[r][:].indirect(offsets[:, j * columns:(j + 1) * columns])
            nc.vector.tensor_scalar(x[:], picked, THRESHOLD, LEVEL, ALU.is_ge, ALU.mult)
            x_bf16 = x[:].bitcast(BF16)[:, 1::2]
            for m in range(strips):
                sums = banks[(j % open_pieces) * strips + m]
                nc.tensor.matmul(sums[:], weights[r][:, m * P:(m + 1) * P], x_bf16,
                                 start=(done[j] == 1), stop=(done[j] == blocks))
                if done[j] == blocks:
                    staged = staging.tile([P, PIECE], F32, name="staged")
                    if j == pieces - 1 and m % 2 == 1:
                        nc.vector.tensor_copy(staged[:], sums[:])
                    else:
                        nc.scalar.copy(staged[:], sums[:])
                    nc.sync.dma_start(out[m * P:(m + 1) * P, j * PIECE:(j + 1) * PIECE], staged[:])
